import numpy as np
import ml_dtypes


def mxq(x, axis, fmt="e4m3"):
    dtype, down = {"e4m3": (ml_dtypes.float8_e4m3fn, 7), "e5m2": (ml_dtypes.float8_e5m2, 14)}[fmt]
    v = np.moveaxis(np.asarray(x, np.float32).astype(ml_dtypes.bfloat16).astype(np.float64), axis, -1)
    blocks = v.reshape(v.shape[:-1] + (-1, 32))
    amax = np.abs(blocks).max(-1, keepdims=True)
    byte = np.maximum(np.where(amax > 0, np.frexp(amax)[1] - 1 + 127, 0) - down, 1)
    scale = np.exp2(byte - 127.0)
    codes = (blocks / scale).astype(np.float32).astype(dtype).astype(np.float64)
    return np.moveaxis((codes * scale).reshape(v.shape), -1, axis)


WIDE = False


def mx_kscale(k):
    if not WIDE:
        return np.ones(k)
    levels = np.array([10, -10, 5, -5, 0])
    if k % 512:
        return np.exp2(np.random.permutation(np.resize(levels, k // 32))).repeat(32)
    a = np.empty((k // 512, 16))
    for p in range(k // 512):
        a[p, :8] = np.random.permutation(np.resize(levels, 8))
        for g in range(8):
            far = levels[np.abs(levels - a[p, g]) >= 10]
            a[p, g + 8] = far[np.random.randint(len(far))]
    return np.exp2(a.ravel()).repeat(32)


def f64(x):
    return np.asarray(x).astype(np.float64)


def striped(idx):
    return np.tile(idx.reshape(-1, 16).T, (8, 1)).astype(np.uint16)


def unstriped(offs):
    return offs[:16].T.reshape(-1).astype(np.int64)


def striped8(idx):
    return np.concatenate([x.reshape(-1, 16).T for x in idx]).astype(np.uint16)


def runs(offs, k):
    lists = np.stack([offs[16 * r : 16 * r + 16].T.reshape(-1) for r in range(8)]).astype(np.int64)
    return lists[np.arange(k) % 512 // 64]


def pack_weight(w):
    k, n = w.shape
    w = f64(np.asarray(w, np.float32).astype(ml_dtypes.bfloat16)).reshape(k // 32, 32, n)
    amax = np.abs(w).max(1)
    byte = np.clip(np.where(amax > 0, np.frexp(amax)[1] - 1 + 127 - 7, 1), 1, 254)
    scaled = (w * np.exp2(127.0 - byte)[:, None, :]).reshape(k, n).astype(np.float32)
    words = np.ascontiguousarray(scaled.reshape(k // 512, 128, 4, n).transpose(0, 1, 3, 2)).astype(ml_dtypes.float8_e4m3fn).view(np.uint8)
    return words, np.ascontiguousarray(byte.astype(np.uint8).reshape(k // 512, 16, n))


def unpack_weight(words, scales):
    g, p, n, _ = words.shape
    vals = np.ascontiguousarray(words).view(ml_dtypes.float8_e4m3fn).astype(np.float64) * np.repeat(np.exp2(scales.astype(np.float64) - 127.0), 8, axis=1)[..., None]
    return vals.transpose(0, 1, 3, 2).reshape(g * 512, n)


K, T, S, N, W = 512, 2048, 256, 512, 128


def setup_inputs():
    n = np.random.standard_normal
    s = mx_kscale(K)[:, None]
    packed_xT = pack_weight(n((K, T)) * s)
    perm = np.random.permutation(S)
    return {
        "x_words": packed_xT[0],
        "x_scales": packed_xT[1],
        "w1": (n((K, N)) / np.sqrt(2 * K) / s).astype(np.float32),
        "w2": (n((K, N)) / np.sqrt(2 * K) / s).astype(np.float32),
        "offs": striped(np.random.permutation(T)[:S]),
        "hz": striped8(np.random.randint(0, T, (8, S))),
        "n1": striped(perm[:W]),
        "n2": striped(perm[W:]),
    }


def reference(x_words, x_scales, w1, w2, offs, hz, n1, n2):
    xq = unpack_weight(x_words, x_scales)[:, unstriped(offs)]
    x_hz = unpack_weight(x_words, x_scales)[np.arange(K)[:, None], runs(hz, K)]
    h = mxq(f64(w1), 0, "e4m3").T @ xq + mxq(f64(w2), 0, "e4m3").T @ x_hz
    pa = h[:, unstriped(n1)]
    pb = h[:, unstriped(n2)]
    rb = pa - pb
    ra = 0.75 * (pa + pb)
    ds = np.zeros((N, S))
    ds[:, unstriped(n1)] = ra
    out = ds.copy()
    out[:, unstriped(n2)] = rb
    return out

@@ -1,0 +1,118 @@
+from contextlib import ExitStack
+
+import concourse.mybir as mybir
+
+K, T, S, N, W = 512, 2048, 256, 512, 128
+FLOPS = 2 * 2 * K * N * S
+
+F32 = mybir.dt.float32
+BF16 = mybir.dt.bfloat16
+I32 = mybir.dt.int32
+U32 = mybir.dt.uint32
+U16 = mybir.dt.uint16
+U8 = mybir.dt.uint8
+FP8X4 = mybir.dt.float8_e4m3fn_x4
+COPY = mybir.ActivationFunctionType.Copy
+ADD = mybir.AluOpType.add
+SUB = mybir.AluOpType.subtract
+
+P = 128
+PACK = 4
+TILES = N // P
+
+
+def tile_picked_othhaar_none_p_kernel(tc, x_words, x_scales, w1, w2, offs, hz, n1, n2, out):
+    nc = tc.nc
+    with ExitStack() as ctx:
+        lists = ctx.enter_context(tc.tile_pool(name="lists", bufs=1))
+        held = ctx.enter_context(tc.tile_pool(name="held", bufs=1))
+        psum = ctx.enter_context(tc.psum_pool(name="psum", bufs=1))
+
+        hz_t = lists.tile([P, S // 16], U16, name="hz_t")
+        offs_t = lists.tile([P, S // 16], U16, name="offs_t")
+        n1_t = lists.tile([P, W // 16], U16, name="n1_t")
+        n2_t = lists.tile([P, W // 16], U16, name="n2_t")
+
+        byte_table = held.tile([P, T], U8, name="byte_table", align_bytes=64)
+        word_table = held.tile([P, T], U32, name="word_table", align_bytes=64)
+        x_plane = held.tile([P, 2 * S], U8, name="x_plane", align_bytes=64)
+        picked_bytes = held.tile([P, 2 * S], U8, name="picked_bytes", align_bytes=64)
+        picked_words = [held.tile([P, S], U32, name=f"picked_words{i}", align_bytes=64) for i in range(2)]
+
+        nc.vector.memset(byte_table[:].bitcast(I32), 0)
+        nc.vector.memset(x_plane[:].bitcast(I32), 0)
+
+        nc.sync.dma_start(hz_t[:], hz)
+        nc.scalar.dma_start(byte_table[0:P:8, :].bitcast(I32), x_scales[0].bitcast(I32))
+        nc.sync.dma_start(offs_t[:], offs)
+        nc.sync.dma_start(n1_t[:], n1)
+        nc.sync.dma_start(n2_t[:], n2)
+        nc.sync.dma_start(word_table[:].bitcast(I32), x_words[0].rearrange("p c r -> p (c r)").bitcast(I32))
+
+        raw = {}
+        for c0, c1 in ((0, P), (P, 2 * P), (2 * P, N)):
+            for i, w in enumerate((w1, w2)):
+                piece = held.tile([P, PACK, c1 - c0], F32, name=f"raw{i}_{c0}")
+                nc.sync.dma_start(piece[:], w.rearrange("(p j) m -> p j m", j=PACK)[:, :, c0:c1])
+                for t in range(c0 // P, c1 // P):
+                    raw[i, t] = piece[:, :, t * P - c0 : (t + 1) * P - c0]
+
+        picks = (offs_t, hz_t)
+        for i in range(2):
+            nc.vector.tensor_copy(picked_bytes[:, i * S : (i + 1) * S], byte_table[:].indirect(picks[i][:]))
+        for r in range(4):
+            nc.scalar.dma_start(x_plane[r:P:32, :].bitcast(I32), picked_bytes[8 * r : P : 32, :].bitcast(I32))
+        for i in range(2):
+            nc.vector.tensor_copy(picked_words[i][:], word_table[:].indirect(picks[i][:]))
+
+        def product(t):
+            grouped = [held.tile([P, P, PACK], BF16, name=f"grouped{i}_{t}", align_bytes=64) for i in range(2)]
+            codes = [held.tile([P, P], U32, name=f"codes{i}_{t}", align_bytes=64) for i in range(2)]
+            planes = [held.tile([P, P], U8, name=f"planes{i}_{t}", align_bytes=64) for i in range(2)]
+            for i in range(2):
+                dst = grouped[i][:].rearrange("p (c e) j -> p c j e", e=4)
+                src = raw[i, t].rearrange("p j (c e) -> p c j e", e=4)
+                if t == 0 and i == 0:
+                    nc.scalar.copy(dst, src)
+                else:
+                    nc.vector.tensor_copy(dst, src)
+            for i in range(2):
+                nc.vector.quantize_mx(out=codes[i][:].bitcast(FP8X4), scales=planes[i][:], in_=grouped[i][:].rearrange("p c j -> p (c j)"))
+            acc = psum.tile([P, S], F32, name=f"acc{t}")
+            for i in range(2):
+                nc.tensor.matmul_mx(
+                    out=acc[:],
+                    lhsT=codes[i][:].bitcast(FP8X4),
+                    lhsT_scale=planes[i][:],
+                    rhs=picked_words[i][:].bitcast(FP8X4),
+                    rhs_scale=x_plane[:, i * S : (i + 1) * S],
+                    start=(i == 0),
+                    stop=(i == 1),
+                )
+            h = held.tile([P, S], F32, name=f"h{t}")
+            nc.vector.tensor_copy(h[:], acc[:])
+            return h
+
+        def fetch(t, h):
+            pa = held.tile([P, W], F32, name=f"pa{t}")
+            pb = held.tile([P, W], F32, name=f"pb{t}")
+            nc.scalar.activation(pa[:], h[:].indirect(n1_t[:]), COPY)
+            nc.scalar.activation(pb[:], h[:].indirect(n2_t[:]), COPY)
+            total = held.tile([P, W], F32, name=f"total{t}")
+            rb = held.tile([P, W], F32, name=f"rb{t}")
+            nc.vector.tensor_tensor(total[:], pa[:], pb[:], ADD)
+            nc.vector.tensor_tensor(rb[:], pa[:], pb[:], SUB)
+            return total, rb
+
+        def put(t, total, rb):
+            res = held.tile([P, S], F32, name=f"res{t}")
+            nc.scalar.activation(res[:].indirect(n1_t[:]), total[:], COPY, scale=0.75)
+            nc.scalar.activation(res[:].indirect(n2_t[:]), rb[:], COPY)
+            nc.sync.dma_start(out[t * P : (t + 1) * P, :], res[:])
+
+        pending = fetch(0, product(0))
+        for t in range(1, TILES):
+            ahead = fetch(t, product(t))
+            put(t - 1, *pending)
+            pending = ahead
+        put(TILES - 1, *pending)

@@ -33,51 +33,66 @@ def tile_picked_othhaar_none_p_kernel(tc, x_words, x_scales, w1, w2, offs, hz, n
         n1_t = lists.tile([P, W // 16], U16, name="n1_t")
         n2_t = lists.tile([P, W // 16], U16, name="n2_t")
 
-        byte_table = held.tile([P, T], U8, name="byte_table", align_bytes=64)
+        byte_table = held.tile([P, T], U8, name="byte_table", tag="bytes_then_weights", align_bytes=64)
         word_table = held.tile([P, T], U32, name="word_table", align_bytes=64)
         x_plane = held.tile([P, 2 * S], U8, name="x_plane", align_bytes=64)
         picked_bytes = held.tile([P, 2 * S], U8, name="picked_bytes", align_bytes=64)
         picked_words = [held.tile([P, S], U32, name=f"picked_words{i}", align_bytes=64) for i in range(2)]
 
         nc.vector.memset(byte_table[:].bitcast(I32), 0)
-        nc.vector.memset(x_plane[:].bitcast(I32), 0)
+        nc.gpsimd.memset(x_plane[:].bitcast(I32), 0)
 
         nc.sync.dma_start(hz_t[:], hz)
-        nc.scalar.dma_start(byte_table[0:P:8, :].bitcast(I32), x_scales[0].bitcast(I32))
+        nc.sync.dma_start(byte_table[0:P:8, :].bitcast(I32), x_scales[0].bitcast(I32))
         nc.sync.dma_start(offs_t[:], offs)
         nc.sync.dma_start(n1_t[:], n1)
         nc.sync.dma_start(n2_t[:], n2)
-        nc.sync.dma_start(word_table[:].bitcast(I32), x_words[0].rearrange("p c r -> p (c r)").bitcast(I32))
 
         raw = {}
-        for c0, c1 in ((0, P), (P, 2 * P), (2 * P, N)):
-            for i, w in enumerate((w1, w2)):
-                piece = held.tile([P, PACK, c1 - c0], F32, name=f"raw{i}_{c0}")
-                nc.sync.dma_start(piece[:], w.rearrange("(p j) m -> p j m", j=PACK)[:, :, c0:c1])
-                for t in range(c0 // P, c1 // P):
-                    raw[i, t] = piece[:, :, t * P - c0 : (t + 1) * P - c0]
+
+        def load_columns(piece, i, c0, c1):
+            nc.sync.dma_start(piece, (w1, w2)[i].rearrange("(p j) m -> p j m", j=PACK)[:, :, c0:c1])
+            for t in range(c0 // P, c1 // P):
+                raw[i, t] = piece[:, :, t * P - c0 : (t + 1) * P - c0]
+
+        first = [held.tile([P, PACK, P], F32, name=f"first{i}") for i in range(2)]
+        load_columns(first[0][:], 0, 0, P)
+        nc.sync.dma_start(word_table[:].bitcast(I32), x_words[0].rearrange("p c r -> p (c r)").bitcast(I32))
+        load_columns(first[1][:], 1, 0, P)
+        second = held.tile([P, PACK, P], F32, name="second")
+        load_columns(second[:], 0, P, 2 * P)
 
         picks = (offs_t, hz_t)
         for i in range(2):
             nc.vector.tensor_copy(picked_bytes[:, i * S : (i + 1) * S], byte_table[:].indirect(picks[i][:]))
         for r in range(4):
-            nc.scalar.dma_start(x_plane[r:P:32, :].bitcast(I32), picked_bytes[8 * r : P : 32, :].bitcast(I32))
+            nc.sync.dma_start(x_plane[r:P:32, :].bitcast(I32), picked_bytes[8 * r : P : 32, :].bitcast(I32))
+
+        blocks = [(i, t) for t in range(1, TILES) for i in range(2)][1:]
+        later = held.tile([P, len(blocks) * PACK * P], F32, name="later", tag="bytes_then_weights", align_bytes=64)
+        for n, (i, t) in enumerate(blocks):
+            piece = later[:, n * PACK * P : (n + 1) * PACK * P].rearrange("p (j m) -> p j m", j=PACK)
+            load_columns(piece, i, t * P, (t + 1) * P)
+
         for i in range(2):
             nc.vector.tensor_copy(picked_words[i][:], word_table[:].indirect(picks[i][:]))
 
-        def product(t):
-            grouped = [held.tile([P, P, PACK], BF16, name=f"grouped{i}_{t}", align_bytes=64) for i in range(2)]
-            codes = [held.tile([P, P], U32, name=f"codes{i}_{t}", align_bytes=64) for i in range(2)]
+        def quantise(t):
+            grouped = [held.tile([P, P, PACK], BF16, name=f"grouped{i}_{t}", tag=f"grouped{i}_{t}", align_bytes=64) for i in range(2)]
+            codes = [held.tile([P, P], U32, name=f"codes{i}_{t}", tag=f"codes{i}_{t}", align_bytes=64) for i in range(2)]
             planes = [held.tile([P, P], U8, name=f"planes{i}_{t}", align_bytes=64) for i in range(2)]
             for i in range(2):
                 dst = grouped[i][:].rearrange("p (c e) j -> p c j e", e=4)
                 src = raw[i, t].rearrange("p j (c e) -> p c j e", e=4)
-                if t == 0 and i == 0:
+                if t == 0:
                     nc.scalar.copy(dst, src)
                 else:
                     nc.vector.tensor_copy(dst, src)
             for i in range(2):
                 nc.vector.quantize_mx(out=codes[i][:].bitcast(FP8X4), scales=planes[i][:], in_=grouped[i][:].rearrange("p c j -> p (c j)"))
+            return codes, planes
+
+        def product(t, codes, planes):
             acc = psum.tile([P, S], F32, name=f"acc{t}")
             for i in range(2):
                 nc.tensor.matmul_mx(
@@ -98,21 +113,29 @@ def tile_picked_othhaar_none_p_kernel(tc, x_words, x_scales, w1, w2, offs, hz, n
             pb = held.tile([P, W], F32, name=f"pb{t}")
             nc.scalar.activation(pa[:], h[:].indirect(n1_t[:]), COPY)
             nc.scalar.activation(pb[:], h[:].indirect(n2_t[:]), COPY)
-            total = held.tile([P, W], F32, name=f"total{t}")
-            rb = held.tile([P, W], F32, name=f"rb{t}")
-            nc.vector.tensor_tensor(total[:], pa[:], pb[:], ADD)
-            nc.vector.tensor_tensor(rb[:], pa[:], pb[:], SUB)
-            return total, rb
+            return pa, pb
 
-        def put(t, total, rb):
+        def put_sum(t, pa, pb):
+            total = held.tile([P, W], F32, name=f"total{t}", tag=f"grouped1_{t + 1}" if t > 0 else "total0", align_bytes=64)
             res = held.tile([P, S], F32, name=f"res{t}")
+            nc.vector.tensor_tensor(total[:], pa[:], pb[:], ADD)
             nc.scalar.activation(res[:].indirect(n1_t[:]), total[:], COPY, scale=0.75)
+            return res
+
+        def put_difference(t, pa, pb, res):
+            rb = held.tile([P, W], F32, name=f"rb{t}", tag=f"codes1_{t + 1}", align_bytes=64)
+            nc.vector.tensor_tensor(rb[:], pa[:], pb[:], SUB)
             nc.scalar.activation(res[:].indirect(n2_t[:]), rb[:], COPY)
             nc.sync.dma_start(out[t * P : (t + 1) * P, :], res[:])
 
-        pending = fetch(0, product(0))
+        pair = fetch(0, product(0, *quantise(0)))
+        res = put_sum(0, *pair)
+        weights = quantise(1)
         for t in range(1, TILES):
-            ahead = fetch(t, product(t))
-            put(t - 1, *pending)
-            pending = ahead
-        put(TILES - 1, *pending)
+            ahead = fetch(t, product(t, *weights))
+            put_difference(t - 1, *pair, res)
+            pair = ahead
+            if t + 1 < TILES:
+                weights = quantise(t + 1)
+            res = put_sum(t, *pair)
+        put_difference(TILES - 1, *pair, res)

@@ -50,25 +50,26 @@ def tile_picked_othhaar_none_p_kernel(tc, x_words, x_scales, w1, w2, offs, hz, n
 
         raw = {}
 
-        def load_columns(piece, i, c0, c1):
-            nc.sync.dma_start(piece, (w1, w2)[i].rearrange("(p j) m -> p j m", j=PACK)[:, :, c0:c1])
+        def load_columns(piece, i, c0, c1, queue=nc.sync):
+            queue.dma_start(piece, (w1, w2)[i].rearrange("(p j) m -> p j m", j=PACK)[:, :, c0:c1])
             for t in range(c0 // P, c1 // P):
                 raw[i, t] = piece[:, :, t * P - c0 : (t + 1) * P - c0]
 
         first = [held.tile([P, PACK, P], F32, name=f"first{i}") for i in range(2)]
-        load_columns(first[0][:], 0, 0, P)
+        load_columns(first[0][:], 0, 0, P, nc.scalar)
         nc.sync.dma_start(word_table[:].bitcast(I32), x_words[0].rearrange("p c r -> p (c r)").bitcast(I32))
         load_columns(first[1][:], 1, 0, P)
-        second = held.tile([P, PACK, P], F32, name="second")
-        load_columns(second[:], 0, P, 2 * P)
+        for i in range(2):
+            second = held.tile([P, PACK, P], F32, name=f"second{i}")
+            load_columns(second[:], i, P, 2 * P)
 
         picks = (offs_t, hz_t)
         for i in range(2):
             nc.vector.tensor_copy(picked_bytes[:, i * S : (i + 1) * S], byte_table[:].indirect(picks[i][:]))
         for r in range(4):
-            nc.sync.dma_start(x_plane[r:P:32, :].bitcast(I32), picked_bytes[8 * r : P : 32, :].bitcast(I32))
+            nc.scalar.dma_start(x_plane[r:P:32, :].bitcast(I32), picked_bytes[8 * r : P : 32, :].bitcast(I32))
 
-        blocks = [(i, t) for t in range(1, TILES) for i in range(2)][1:]
+        blocks = [(i, t) for t in range(2, TILES) for i in range(2)]
         later = held.tile([P, len(blocks) * PACK * P], F32, name="later", tag="bytes_then_weights", align_bytes=64)
         for n, (i, t) in enumerate(blocks):
             piece = later[:, n * PACK * P : (n + 1) * PACK * P].rearrange("p (j m) -> p j m", j=PACK)

@@ -18,7 +18,13 @@ SUB = mybir.AluOpType.subtract
 
 P = 128
 PACK = 4
-TILES = N // P
+BLOCKS = N // P
+GROUP = 16
+QUADRANT = 32
+ROW_STEP = 8
+RUN = 4
+EARLY_BLOCKS = 2
+ROUNDED_ON_SCALAR = ((0, 0), (1, 0), (0, 1))
 
 
 def tile_picked_othhaar_none_p_kernel(tc, x_words, x_scales, w1, w2, offs, hz, n1, n2, out):
@@ -28,10 +34,11 @@ def tile_picked_othhaar_none_p_kernel(tc, x_words, x_scales, w1, w2, offs, hz, n
         held = ctx.enter_context(tc.tile_pool(name="held", bufs=1))
         psum = ctx.enter_context(tc.psum_pool(name="psum", bufs=1))
 
-        hz_t = lists.tile([P, S // 16], U16, name="hz_t")
-        offs_t = lists.tile([P, S // 16], U16, name="offs_t")
-        n1_t = lists.tile([P, W // 16], U16, name="n1_t")
-        n2_t = lists.tile([P, W // 16], U16, name="n2_t")
+        hz_list = lists.tile([P, S // GROUP], U16, name="hz_list")
+        offs_list = lists.tile([P, S // GROUP], U16, name="offs_list")
+        n1_list = lists.tile([P, W // GROUP], U16, name="n1_list")
+        n2_list = lists.tile([P, W // GROUP], U16, name="n2_list")
+        picks = (offs_list, hz_list)
 
         byte_table = held.tile([P, T], U8, name="byte_table", tag="bytes_then_weights", align_bytes=64)
         word_table = held.tile([P, T], U32, name="word_table", align_bytes=64)
@@ -42,101 +49,107 @@ def tile_picked_othhaar_none_p_kernel(tc, x_words, x_scales, w1, w2, offs, hz, n
         nc.vector.memset(byte_table[:].bitcast(I32), 0)
         nc.gpsimd.memset(x_plane[:].bitcast(I32), 0)
 
-        nc.sync.dma_start(hz_t[:], hz)
-        nc.sync.dma_start(byte_table[0:P:8, :].bitcast(I32), x_scales[0].bitcast(I32))
-        nc.sync.dma_start(offs_t[:], offs)
-        nc.sync.dma_start(n1_t[:], n1)
-        nc.sync.dma_start(n2_t[:], n2)
+        nc.sync.dma_start(hz_list[:], hz)
+        nc.sync.dma_start(byte_table[0:P:ROW_STEP, :].bitcast(I32), x_scales[0].bitcast(I32))
+        nc.sync.dma_start(offs_list[:], offs)
+        nc.sync.dma_start(n1_list[:], n1)
+        nc.sync.dma_start(n2_list[:], n2)
 
         raw = {}
 
-        def load_columns(piece, i, c0, c1, queue=nc.sync):
-            queue.dma_start(piece, (w1, w2)[i].rearrange("(p j) m -> p j m", j=PACK)[:, :, c0:c1])
-            for t in range(c0 // P, c1 // P):
-                raw[i, t] = piece[:, :, t * P - c0 : (t + 1) * P - c0]
+        def load_weights(piece, i, b, queue):
+            rows = (w1, w2)[i].rearrange("(p j) m -> p j m", j=PACK)
+            queue.dma_start(piece, rows[:, :, b * P : (b + 1) * P])
+            raw[i, b] = piece
 
         first = [held.tile([P, PACK, P], F32, name=f"first{i}") for i in range(2)]
-        load_columns(first[0][:], 0, 0, P, nc.scalar)
+        load_weights(first[0][:], 0, 0, nc.scalar)
         nc.sync.dma_start(word_table[:].bitcast(I32), x_words[0].rearrange("p c r -> p (c r)").bitcast(I32))
-        load_columns(first[1][:], 1, 0, P)
+        load_weights(first[1][:], 1, 0, nc.sync)
         for i in range(2):
             second = held.tile([P, PACK, P], F32, name=f"second{i}")
-            load_columns(second[:], i, P, 2 * P)
+            load_weights(second[:], i, 1, nc.sync)
 
-        picks = (offs_t, hz_t)
         for i in range(2):
             nc.vector.tensor_copy(picked_bytes[:, i * S : (i + 1) * S], byte_table[:].indirect(picks[i][:]))
-        for r in range(4):
-            nc.scalar.dma_start(x_plane[r:P:32, :].bitcast(I32), picked_bytes[8 * r : P : 32, :].bitcast(I32))
+        for r in range(QUADRANT // ROW_STEP):
+            nc.scalar.dma_start(
+                x_plane[r:P:QUADRANT, :].bitcast(I32),
+                picked_bytes[ROW_STEP * r : P : QUADRANT, :].bitcast(I32),
+            )
 
-        blocks = [(i, t) for t in range(2, TILES) for i in range(2)]
-        later = held.tile([P, len(blocks) * PACK * P], F32, name="later", tag="bytes_then_weights", align_bytes=64)
-        for n, (i, t) in enumerate(blocks):
-            piece = later[:, n * PACK * P : (n + 1) * PACK * P].rearrange("p (j m) -> p j m", j=PACK)
-            load_columns(piece, i, t * P, (t + 1) * P)
+        late_pieces = [(i, b) for b in range(EARLY_BLOCKS, BLOCKS) for i in range(2)]
+        late = held.tile([P, len(late_pieces) * PACK * P], F32, name="late", tag="bytes_then_weights", align_bytes=64)
+        for place, (i, b) in enumerate(late_pieces):
+            piece = late[:, place * PACK * P : (place + 1) * PACK * P].rearrange("p (j m) -> p j m", j=PACK)
+            load_weights(piece, i, b, nc.sync)
 
         for i in range(2):
             nc.vector.tensor_copy(picked_words[i][:], word_table[:].indirect(picks[i][:]))
 
-        def quantise(t):
-            grouped = [held.tile([P, P, PACK], BF16, name=f"grouped{i}_{t}", tag=f"grouped{i}_{t}", align_bytes=64) for i in range(2)]
-            codes = [held.tile([P, P], U32, name=f"codes{i}_{t}", tag=f"codes{i}_{t}", align_bytes=64) for i in range(2)]
-            planes = [held.tile([P, P], U8, name=f"planes{i}_{t}", align_bytes=64) for i in range(2)]
+        def quantise(b):
+            grouped = [held.tile([P, P, PACK], BF16, name=f"grouped{i}_{b}", tag=f"grouped{i}_{b}", align_bytes=64) for i in range(2)]
+            words = [held.tile([P, P], U32, name=f"words{i}_{b}", tag=f"words{i}_{b}", align_bytes=64) for i in range(2)]
+            planes = [held.tile([P, P], U8, name=f"planes{i}_{b}", align_bytes=64) for i in range(2)]
             for i in range(2):
-                dst = grouped[i][:].rearrange("p (c e) j -> p c j e", e=4)
-                src = raw[i, t].rearrange("p j (c e) -> p c j e", e=4)
-                if t == 0:
+                dst = grouped[i][:].rearrange("p (c e) j -> p c j e", e=RUN)
+                src = raw[i, b].rearrange("p j (c e) -> p c j e", e=RUN)
+                if (i, b) in ROUNDED_ON_SCALAR:
                     nc.scalar.copy(dst, src)
                 else:
                     nc.vector.tensor_copy(dst, src)
             for i in range(2):
-                nc.vector.quantize_mx(out=codes[i][:].bitcast(FP8X4), scales=planes[i][:], in_=grouped[i][:].rearrange("p c j -> p (c j)"))
-            return codes, planes
+                nc.vector.quantize_mx(
+                    out=words[i][:].bitcast(FP8X4),
+                    scales=planes[i][:],
+                    in_=grouped[i][:].rearrange("p c j -> p (c j)"),
+                )
+            return words, planes
 
-        def product(t, codes, planes):
-            acc = psum.tile([P, S], F32, name=f"acc{t}")
+        def product(b, words, planes):
+            acc = psum.tile([P, S], F32, name=f"acc{b}")
             for i in range(2):
                 nc.tensor.matmul_mx(
                     out=acc[:],
-                    lhsT=codes[i][:].bitcast(FP8X4),
+                    lhsT=words[i][:].bitcast(FP8X4),
                     lhsT_scale=planes[i][:],
                     rhs=picked_words[i][:].bitcast(FP8X4),
                     rhs_scale=x_plane[:, i * S : (i + 1) * S],
                     start=(i == 0),
                     stop=(i == 1),
                 )
-            h = held.tile([P, S], F32, name=f"h{t}")
-            nc.vector.tensor_copy(h[:], acc[:])
+            h = held.tile([P, S], F32, name=f"h{b}", tag=f"h{b}", align_bytes=64)
+            if b == 0:
+                nc.scalar.copy(h[:], acc[:])
+            else:
+                nc.vector.tensor_copy(h[:], acc[:])
             return h
 
-        def fetch(t, h):
-            pa = held.tile([P, W], F32, name=f"pa{t}")
-            pb = held.tile([P, W], F32, name=f"pb{t}")
-            nc.scalar.activation(pa[:], h[:].indirect(n1_t[:]), COPY)
-            nc.scalar.activation(pb[:], h[:].indirect(n2_t[:]), COPY)
+        def fetch(b, h):
+            pa = held.tile([P, W], F32, name=f"pa{b}")
+            pb = held.tile([P, W], F32, name=f"pb{b}")
+            nc.scalar.activation(pa[:], h[:].indirect(n1_list[:]), COPY)
+            nc.scalar.activation(pb[:], h[:].indirect(n2_list[:]), COPY)
             return pa, pb
 
-        def put_sum(t, pa, pb):
-            total = held.tile([P, W], F32, name=f"total{t}", tag=f"grouped1_{t + 1}" if t > 0 else "total0", align_bytes=64)
-            res = held.tile([P, S], F32, name=f"res{t}")
+        def put_sum(b, pa, pb, buffer):
+            total = held.tile([P, W], F32, name=f"total{b}", tag=buffer, align_bytes=64)
+            result = held.tile([P, S], F32, name=f"result{b}")
             nc.vector.tensor_tensor(total[:], pa[:], pb[:], ADD)
-            nc.scalar.activation(res[:].indirect(n1_t[:]), total[:], COPY, scale=0.75)
-            return res
+            nc.scalar.activation(result[:].indirect(n1_list[:]), total[:], COPY, scale=0.75)
+            return result
 
-        def put_difference(t, pa, pb, res):
-            rb = held.tile([P, W], F32, name=f"rb{t}", tag=f"codes1_{t + 1}", align_bytes=64)
+        def put_difference(b, pa, pb, result, buffer):
+            rb = held.tile([P, W], F32, name=f"rb{b}", tag=buffer, align_bytes=64)
             nc.vector.tensor_tensor(rb[:], pa[:], pb[:], SUB)
-            nc.scalar.activation(res[:].indirect(n2_t[:]), rb[:], COPY)
-            nc.sync.dma_start(out[t * P : (t + 1) * P, :], res[:])
+            nc.scalar.activation(result[:].indirect(n2_list[:]), rb[:], COPY)
+            nc.sync.dma_start(out[b * P : (b + 1) * P, :], result[:])
 
-        pair = fetch(0, product(0, *quantise(0)))
-        res = put_sum(0, *pair)
-        weights = quantise(1)
-        for t in range(1, TILES):
-            ahead = fetch(t, product(t, *weights))
-            put_difference(t - 1, *pair, res)
-            pair = ahead
-            if t + 1 < TILES:
-                weights = quantise(t + 1)
-            res = put_sum(t, *pair)
-        put_difference(TILES - 1, *pair, res)
+        for a in range(0, BLOCKS, 2):
+            b = a + 1
+            pair_a = fetch(a, product(a, *quantise(a)))
+            pair_b = fetch(b, product(b, *quantise(b)))
+            result_a = put_sum(a, *pair_a, f"words1_{b}")
+            result_b = put_sum(b, *pair_b, f"total{b}")
+            put_difference(a, *pair_a, result_a, f"h{b}")
+            put_difference(b, *pair_b, result_b, f"rb{b}")

from contextlib import ExitStack

import concourse.mybir as mybir

K, T, S, N, W = 512, 2048, 256, 512, 128
FLOPS = 2 * 2 * K * N * S

F32 = mybir.dt.float32
BF16 = mybir.dt.bfloat16
I32 = mybir.dt.int32
U32 = mybir.dt.uint32
U16 = mybir.dt.uint16
U8 = mybir.dt.uint8
FP8X4 = mybir.dt.float8_e4m3fn_x4
COPY = mybir.ActivationFunctionType.Copy
ADD = mybir.AluOpType.add
SUB = mybir.AluOpType.subtract

P = 128
PACK = 4
BLOCKS = N // P
GROUP = 16
QUADRANT = 32
ROW_STEP = 8
RUN = 4
EARLY_BLOCKS = 2
ROUNDED_ON_SCALAR = ((0, 0), (1, 0), (0, 1))


def tile_picked_othhaar_none_p_kernel(tc, x_words, x_scales, w1, w2, offs, hz, n1, n2, out):
    nc = tc.nc
    with ExitStack() as ctx:
        lists = ctx.enter_context(tc.tile_pool(name="lists", bufs=1))
        held = ctx.enter_context(tc.tile_pool(name="held", bufs=1))
        psum = ctx.enter_context(tc.psum_pool(name="psum", bufs=1))

        hz_list = lists.tile([P, S // GROUP], U16, name="hz_list")
        offs_list = lists.tile([P, S // GROUP], U16, name="offs_list")
        n1_list = lists.tile([P, W // GROUP], U16, name="n1_list")
        n2_list = lists.tile([P, W // GROUP], U16, name="n2_list")
        picks = (offs_list, hz_list)

        byte_table = held.tile([P, T], U8, name="byte_table", tag="bytes_then_weights", align_bytes=64)
        word_table = held.tile([P, T], U32, name="word_table", align_bytes=64)
        x_plane = held.tile([P, 2 * S], U8, name="x_plane", align_bytes=64)
        picked_bytes = held.tile([P, 2 * S], U8, name="picked_bytes", align_bytes=64)
        picked_words = [held.tile([P, S], U32, name=f"picked_words{i}", align_bytes=64) for i in range(2)]

        nc.vector.memset(byte_table[:].bitcast(I32), 0)
        nc.gpsimd.memset(x_plane[:].bitcast(I32), 0)

        nc.sync.dma_start(hz_list[:], hz)
        nc.sync.dma_start(byte_table[0:P:ROW_STEP, :].bitcast(I32), x_scales[0].bitcast(I32))
        nc.sync.dma_start(offs_list[:], offs)
        nc.sync.dma_start(n1_list[:], n1)
        nc.sync.dma_start(n2_list[:], n2)

        raw = {}

        def load_weights(piece, i, b, queue):
            rows = (w1, w2)[i].rearrange("(p j) m -> p j m", j=PACK)
            queue.dma_start(piece, rows[:, :, b * P : (b + 1) * P])
            raw[i, b] = piece

        first = [held.tile([P, PACK, P], F32, name=f"first{i}") for i in range(2)]
        load_weights(first[0][:], 0, 0, nc.scalar)
        nc.sync.dma_start(word_table[:].bitcast(I32), x_words[0].rearrange("p c r -> p (c r)").bitcast(I32))
        load_weights(first[1][:], 1, 0, nc.sync)
        for i in range(2):
            second = held.tile([P, PACK, P], F32, name=f"second{i}")
            load_weights(second[:], i, 1, nc.sync)

        for i in range(2):
            nc.vector.tensor_copy(picked_bytes[:, i * S : (i + 1) * S], byte_table[:].indirect(picks[i][:]))
        for r in range(QUADRANT // ROW_STEP):
            nc.scalar.dma_start(
                x_plane[r:P:QUADRANT, :].bitcast(I32),
                picked_bytes[ROW_STEP * r : P : QUADRANT, :].bitcast(I32),
            )

        late_pieces = [(i, b) for b in range(EARLY_BLOCKS, BLOCKS) for i in range(2)]
        late = held.tile([P, len(late_pieces) * PACK * P], F32, name="late", tag="bytes_then_weights", align_bytes=64)
        for place, (i, b) in enumerate(late_pieces):
            piece = late[:, place * PACK * P : (place + 1) * PACK * P].rearrange("p (j m) -> p j m", j=PACK)
            load_weights(piece, i, b, nc.sync)

        for i in range(2):
            nc.vector.tensor_copy(picked_words[i][:], word_table[:].indirect(picks[i][:]))

        def quantise(b):
            grouped = [held.tile([P, P, PACK], BF16, name=f"grouped{i}_{b}", tag=f"grouped{i}_{b}", align_bytes=64) for i in range(2)]
            words = [held.tile([P, P], U32, name=f"words{i}_{b}", tag=f"words{i}_{b}", align_bytes=64) for i in range(2)]
            planes = [held.tile([P, P], U8, name=f"planes{i}_{b}", align_bytes=64) for i in range(2)]
            for i in range(2):
                dst = grouped[i][:].rearrange("p (c e) j -> p c j e", e=RUN)
                src = raw[i, b].rearrange("p j (c e) -> p c j e", e=RUN)
                if (i, b) in ROUNDED_ON_SCALAR:
                    nc.scalar.copy(dst, src)
                else:
                    nc.vector.tensor_copy(dst, src)
            for i in range(2):
                nc.vector.quantize_mx(
                    out=words[i][:].bitcast(FP8X4),
                    scales=planes[i][:],
                    in_=grouped[i][:].rearrange("p c j -> p (c j)"),
                )
            return words, planes

        def product(b, words, planes):
            acc = psum.tile([P, S], F32, name=f"acc{b}")
            for i in range(2):
                nc.tensor.matmul_mx(
                    out=acc[:],
                    lhsT=words[i][:].bitcast(FP8X4),
                    lhsT_scale=planes[i][:],
                    rhs=picked_words[i][:].bitcast(FP8X4),
                    rhs_scale=x_plane[:, i * S : (i + 1) * S],
                    start=(i == 0),
                    stop=(i == 1),
                )
            h = held.tile([P, S], F32, name=f"h{b}", tag=f"h{b}", align_bytes=64)
            if b == 0:
                nc.scalar.copy(h[:], acc[:])
            else:
                nc.vector.tensor_copy(h[:], acc[:])
            return h

        def fetch(b, h):
            pa = held.tile([P, W], F32, name=f"pa{b}")
            pb = held.tile([P, W], F32, name=f"pb{b}")
            nc.scalar.activation(pa[:], h[:].indirect(n1_list[:]), COPY)
            nc.scalar.activation(pb[:], h[:].indirect(n2_list[:]), COPY)
            return pa, pb

        def put_sum(b, pa, pb, buffer):
            total = held.tile([P, W], F32, name=f"total{b}", tag=buffer, align_bytes=64)
            result = held.tile([P, S], F32, name=f"result{b}")
            nc.vector.tensor_tensor(total[:], pa[:], pb[:], ADD)
            nc.scalar.activation(result[:].indirect(n1_list[:]), total[:], COPY, scale=0.75)
            return result

        def put_difference(b, pa, pb, result, buffer):
            rb = held.tile([P, W], F32, name=f"rb{b}", tag=buffer, align_bytes=64)
            nc.vector.tensor_tensor(rb[:], pa[:], pb[:], SUB)
            nc.scalar.activation(result[:].indirect(n2_list[:]), rb[:], COPY)
            nc.sync.dma_start(out[b * P : (b + 1) * P, :], result[:])

        for a in range(0, BLOCKS, 2):
            b = a + 1
            pair_a = fetch(a, product(a, *quantise(a)))
            pair_b = fetch(b, product(b, *quantise(b)))
            result_a = put_sum(a, *pair_a, f"words1_{b}")
            result_b = put_sum(b, *pair_b, f"total{b}")
            put_difference(a, *pair_a, result_a, f"h{b}")
            put_difference(b, *pair_b, result_b, f"rb{b}")
